import numpy as np
import ml_dtypes

BF16 = ml_dtypes.bfloat16


def bf(x):
    return np.asarray(x, np.float32).astype(BF16)


def f32(x):
    return np.asarray(x, np.float32)


def f64(x):
    return np.asarray(x).astype(np.float64)


def striped(idx):
    return np.tile(idx.reshape(-1, 16).T, (8, 1))


def rows(idx, k):
    return np.tile(idx, (k, 1))


def look(tab, idx):
    return np.take_along_axis(f64(tab), rows(idx, len(tab)), axis=1)


K, S, V, N = 256, 2048, 1536, 1536


def setup_inputs():
    return {"tab": f32(np.random.standard_normal((K, S))), "y": f32(np.random.standard_normal((K, V))), "offs": striped(np.random.permutation(S)[:N])}


def reference(tab, y, offs):
    idx = offs[:16].T.reshape(-1)
    t = look(tab, idx)
    x = t**2 * f64(y)
    return x

@@ -1,0 +1,42 @@
+import concourse.mybir as mybir
+
+F32 = mybir.dt.float32
+U16 = mybir.dt.uint16
+SQUARE = mybir.ActivationFunctionType.Square
+MULT = mybir.AluOpType.mult
+
+P = 128
+PER_COLUMN = 16
+PIECE = 512
+
+
+def tile_lookup_gate_sq_out_kernel(tc, tab, y, offs, out):
+    nc = tc.nc
+    rows, table_columns = tab.shape
+    entries = y.shape[1]
+    blocks = rows // P
+
+    with tc.tile_pool(name="held", bufs=1) as held:
+        offsets = held.tile([P, entries // PER_COLUMN], U16, name="offsets")
+        nc.sync.dma_start(offsets[:], offs)
+
+        windows, streams = [], []
+        for b in range(blocks):
+            block_rows = slice(b * P, (b + 1) * P)
+            window = held.tile([P, table_columns], F32, name=f"window{b}")
+            nc.sync.dma_start(window[:], tab[block_rows, :])
+            windows.append(window)
+            stream = held.tile([P, entries], F32, name=f"stream{b}")
+            nc.sync.dma_start(stream[:], y[block_rows, :])
+            streams.append(stream)
+
+        for b in range(blocks):
+            block_rows = slice(b * P, (b + 1) * P)
+            for start in range(0, entries, PIECE):
+                piece = slice(start, start + PIECE)
+                piece_offsets = offsets[:, start // PER_COLUMN : (start + PIECE) // PER_COLUMN]
+                squares = held.tile([P, PIECE], F32, name=f"squares{b}_{start}")
+                nc.scalar.activation(squares[:], windows[b][:].indirect(piece_offsets), SQUARE)
+                gated = held.tile([P, PIECE], F32, name=f"gated{b}_{start}")
+                nc.vector.tensor_tensor(gated[:], squares[:], streams[b][:, piece], MULT)
+                nc.sync.dma_start(out[block_rows, piece], gated[:])

@@ -17,6 +17,11 @@ def tile_lookup_gate_sq_out_kernel(tc, tab, y, offs, out):
     blocks = rows // P
 
     with tc.tile_pool(name="held", bufs=1) as held:
+        ones = held.tile([P, 1], F32, name="ones")
+        nc.vector.memset(ones[:], 1.0)
+        warm = held.tile([P, 1], F32, name="warm")
+        nc.scalar.activation(warm[:], ones[:], SQUARE)
+
         offsets = held.tile([P, entries // PER_COLUMN], U16, name="offsets")
         nc.sync.dma_start(offsets[:], offs)
 

@@ -37,11 +37,14 @@ def tile_lookup_gate_sq_out_kernel(tc, tab, y, offs, out):
 
         for b in range(blocks):
             block_rows = slice(b * P, (b + 1) * P)
-            for start in range(0, entries, PIECE):
-                piece = slice(start, start + PIECE)
-                piece_offsets = offsets[:, start // PER_COLUMN : (start + PIECE) // PER_COLUMN]
-                squares = held.tile([P, PIECE], F32, name=f"squares{b}_{start}")
+            starts = list(range(0, entries, PIECE))
+            if b == blocks - 1:
+                starts += [entries - PIECE // 2, entries - PIECE // 4]
+            for start, end in zip(starts, starts[1:] + [entries]):
+                piece = slice(start, end)
+                piece_offsets = offsets[:, start // PER_COLUMN : end // PER_COLUMN]
+                squares = held.tile([P, end - start], F32, name=f"squares{b}_{start}")
                 nc.scalar.activation(squares[:], windows[b][:].indirect(piece_offsets), SQUARE)
-                gated = held.tile([P, PIECE], F32, name=f"gated{b}_{start}")
+                gated = held.tile([P, end - start], F32, name=f"gated{b}_{start}")
                 nc.vector.tensor_tensor(gated[:], squares[:], streams[b][:, piece], MULT)
                 nc.sync.dma_start(out[block_rows, piece], gated[:])

@@ -27,12 +27,12 @@ def tile_lookup_gate_sq_out_kernel(tc, tab, y, offs, out):
 
         windows, streams = [], []
         for b in range(blocks):
-            block_rows = slice(b * P, (b + 1) * P)
             window = held.tile([P, table_columns], F32, name=f"window{b}")
-            nc.sync.dma_start(window[:], tab[block_rows, :])
+            nc.sync.dma_start(window[:], tab[b * P : (b + 1) * P, :])
             windows.append(window)
+        for b in range(blocks):
             stream = held.tile([P, entries], F32, name=f"stream{b}")
-            nc.sync.dma_start(stream[:], y[block_rows, :])
+            nc.sync.dma_start(stream[:], y[b * P : (b + 1) * P, :])
             streams.append(stream)
 
         for b in range(blocks):

import concourse.mybir as mybir

F32 = mybir.dt.float32
U16 = mybir.dt.uint16
SQUARE = mybir.ActivationFunctionType.Square
MULT = mybir.AluOpType.mult

P = 128
PER_COLUMN = 16
PIECE = 512


def tile_lookup_gate_sq_out_kernel(tc, tab, y, offs, out):
    nc = tc.nc
    rows, table_columns = tab.shape
    entries = y.shape[1]
    blocks = rows // P

    with tc.tile_pool(name="held", bufs=1) as held:
        ones = held.tile([P, 1], F32, name="ones")
        nc.vector.memset(ones[:], 1.0)
        warm = held.tile([P, 1], F32, name="warm")
        nc.scalar.activation(warm[:], ones[:], SQUARE)

        offsets = held.tile([P, entries // PER_COLUMN], U16, name="offsets")
        nc.sync.dma_start(offsets[:], offs)

        windows, streams = [], []
        for b in range(blocks):
            window = held.tile([P, table_columns], F32, name=f"window{b}")
            nc.sync.dma_start(window[:], tab[b * P : (b + 1) * P, :])
            windows.append(window)
        for b in range(blocks):
            stream = held.tile([P, entries], F32, name=f"stream{b}")
            nc.sync.dma_start(stream[:], y[b * P : (b + 1) * P, :])
            streams.append(stream)

        for b in range(blocks):
            block_rows = slice(b * P, (b + 1) * P)
            starts = list(range(0, entries, PIECE))
            if b == blocks - 1:
                starts += [entries - PIECE // 2, entries - PIECE // 4]
            for start, end in zip(starts, starts[1:] + [entries]):
                piece = slice(start, end)
                piece_offsets = offsets[:, start // PER_COLUMN : end // PER_COLUMN]
                squares = held.tile([P, end - start], F32, name=f"squares{b}_{start}")
                nc.scalar.activation(squares[:], windows[b][:].indirect(piece_offsets), SQUARE)
                gated = held.tile([P, end - start], F32, name=f"gated{b}_{start}")
                nc.vector.tensor_tensor(gated[:], squares[:], streams[b][:, piece], MULT)
                nc.sync.dma_start(out[block_rows, piece], gated[:])
